import numpy as np, ml_dtypes
CORES = [65,73,81,89,97,105,113,121]
N = 8
C = 1024
SIGN = [[1,1,1,1,1,1,1,1],[1,-1,1,-1,1,-1,1,-1],[1,1,-1,-1,1,1,-1,-1],[1,-1,-1,1,1,-1,-1,1],[1,1,1,1,-1,-1,-1,-1],[1,-1,1,-1,-1,1,-1,1],[1,1,-1,-1,-1,-1,1,1],[1,-1,-1,1,-1,1,1,-1]]
def setup_inputs(rng):
    return {"x": rng.standard_normal((N, 128, C), dtype=np.float32).astype(ml_dtypes.bfloat16)}
def setup_inputs_big(rng):
    d = setup_inputs(rng)
    for k in ("x",): d[k] = (d[k].astype(np.float32) * 1048576.0).astype(d[k].dtype)
    return d
def setup_inputs_small(rng):
    d = setup_inputs(rng)
    for k in ("x",): d[k] = (d[k].astype(np.float32) * (1 / 1048576.0)).astype(d[k].dtype)
    return d
def setup_inputs_apart(rng):
    d = setup_inputs(rng)
    f = (10.0 ** rng.permutation(np.linspace(-1.5, 1.5, N))).astype(np.float32).reshape(N, 1, 1)
    for k in ("x",): d[k] = (d[k].astype(np.float32) * f).astype(d[k].dtype)
    return d
def reference(x):
    X = x.astype(np.float64)
    y = np.stack([sum(SIGN[r][j] * X[j] for j in range(N)) for r in range(N)])
    return {"y": y.astype(ml_dtypes.bfloat16)}

@@ -1,0 +1,189 @@
+import comms_topo
+from concourse.bass import DstId, RemoteDMATransfer
+
+N = 8
+ROWS = 128
+C = 1024
+
+
+def _all_cores():
+    return range(comms_topo.CHIPS * comms_topo.CORES_PER_CHIP)
+
+
+def _port_owners(ch):
+    far = [c for c in _all_cores() if comms_topo.mates(ch, comms_topo.chip(c))][0]
+    return [c for c in _all_cores() if comms_topo.chip(c) == ch and comms_topo.may_write(c, far)]
+
+
+H = len(_port_owners(0))
+NP = N * H
+W = C // NP
+Q = ROWS // N
+SW = N * W
+XR = ROWS // NP
+
+SCRATCH = {
+    "Xd": ("dram", [NP, ROWS, W], "bfloat16"),
+    "Hb": ("dram", [N, ROWS, W], "bfloat16"),
+    "L": ("dram", [N, ROWS, W], "bfloat16"),
+    "S": ("sbuf", [ROWS, SW], "bfloat16"),
+    "A": ("sbuf", [ROWS, ROWS + 1], "bfloat16"),
+    "Z": ("dram", [N, Q * (ROWS + 1)], "bfloat16"),
+    "Mx": ("sbuf", [ROWS, ROWS], "bfloat16"),
+    "P": ("psum", [ROWS, SW], "float32"),
+    "O": ("sbuf", [ROWS, SW], "bfloat16"),
+    "Od": ("dram", [N, ROWS, W], "bfloat16"),
+    "Yd": ("dram", [NP, ROWS, W], "bfloat16"),
+}
+SEMAPHORES = ["ldA", "ldB", "sent", "hb", "arr", "ms", "zs", "mr", "sl", "mm", "cp", "bo", "yarr", "st"]
+
+
+def _bits(mask):
+    return [1 << b for b in range(16) if (mask >> b) & 1]
+
+
+def _fused(g, core, topo, items, local_sem):
+    groups = {}
+    for it in items:
+        groups.setdefault(topo.mask(core, it[0]), []).append(it)
+    used = set()
+    trs = []
+    for m in sorted(groups, key=lambda m: len(_bits(m))):
+        free = [e for e in _bits(m) if e not in used]
+        grp = groups[m]
+        step = max(1, len(free) // len(grp))
+        for i, (dstc, src, dst, sem) in enumerate(grp):
+            e = free[i * step]
+            used.add(e)
+            rid, pid, _se = topo.addr(dstc)
+            trs.append(RemoteDMATransfer(dst_ids=[DstId(rid=rid, pnc=pid)], dma_engine_mask=e,
+                                         remote_sem=sem, src=src, dst=dst))
+    g.remote_dma_fused(trs, local_sem=local_sem)
+    return len(trs)
+
+
+def _runs(rs):
+    rs = list(rs)
+    out = []
+    while rs:
+        if len(rs) == 1:
+            out.append((rs[0], 1, 1))
+            break
+        step = rs[1] - rs[0]
+        n = 2
+        while n < len(rs) and rs[n] - rs[n - 1] == step:
+            n += 1
+        out.append((rs[0], step, n))
+        rs = rs[n:]
+    return out
+
+
+def _build_matrix(g, T, order):
+    sign = T.tables["SIGN"]
+    v = g.vector
+    n = [0]
+
+    def fill(p0, p1, rs, val):
+        for (a, step, cnt) in _runs(rs):
+            v.memset(T.A[p0:p1, Q * a:Q * (a + step * (cnt - 1)) + 1:Q * step], val).then_inc(T.sem.ms, 1)
+            n[0] += 1
+
+    def layer():
+        v.wait_ge(T.sem.ms, n[0])
+
+    v.memset(T.A[:, :], 0.0).then_inc(T.sem.ms, 1)
+    n[0] += 1
+    layer()
+    fill(0, ROWS, list(range(N)), 1.0)
+    layer()
+    for m in range(N // 2):
+        up = order[2 * m + 1]
+        fill(2 * Q * m, 2 * Q * (m + 1), [r for r in range(N) if sign[r][up] < 0], -1.0)
+    layer()
+    for m in range(N // 2):
+        lo, up = order[2 * m], order[2 * m + 1]
+        for val in (1, -1):
+            rs = [r for r in range(N) if sign[r][lo] == val and sign[r][up] != val]
+            if rs:
+                fill(2 * Q * m, 2 * Q * m + Q, rs, float(val))
+    s = g.scalar
+    s.wait_ge(T.sem.ms, n[0])
+    s.dma_start(T.Z[:, :], T.A[:, :]).then_inc(T.sem.zs, 16)
+    s.wait_ge(T.sem.zs, 16)
+    s.dma_start(T.Mx[:, :], T.Z[:, 0:Q * ROWS]).then_inc(T.sem.mr, 16)
+
+
+def rank_program(g, core, T, topo):
+    cores = list(T.cores)
+    chips = [topo.chip(c) for c in cores]
+    g0 = [r for r in range(N) if chips[r] == chips[0] or topo.same_plane(chips[r], chips[0])]
+    g1 = [r for r in range(N) if r not in g0]
+    order = g0 + g1
+    pos = {r: i for i, r in enumerate(order)}
+    helpers = {r: [c for c in _port_owners(chips[r]) if c not in cores] for r in range(N)}
+
+    rank = T.rank_of(core)
+    if rank is not None:
+        mine, other = (g0, g1) if rank in g0 else (g1, g0)
+        hs = helpers[rank]
+
+        def half(grp):
+            return H * pos[grp[0]], H * pos[grp[-1]] + H
+
+        a0, a1 = half(other)
+        b0, b1 = half(mine)
+        g.sync.dma_start(T.Xd[a0:a1], T.x[XR * a0:XR * a1, :]).then_inc(T.sem.ldA, 16)
+        g.scalar.dma_start(T.Xd[b0:b1], T.x[XR * b0:XR * b1, :]).then_inc(T.sem.ldB, 16)
+        seen = {}
+        key = {}
+        for h in range(H):
+            d = topo.die(hs[h])
+            key[h] = (seen.get(d, 0), d != topo.die(core))
+            seen[d] = seen.get(d, 0) + 1
+        hord = sorted(range(H), key=lambda h: key[h])
+        sent = 0
+        g.wait_ge(T.sem.ldA, 16)
+        items = [(hs[h], T.Xd[H * pos[p] + h], T.Hb[i], T.sem.hb) for i, p in enumerate(other) for h in hord]
+        sent += _fused(g, core, topo, items, T.sem.sent)
+        g.wait_ge(T.sem.ldB, 16)
+        far = [(helpers[p][h], T.Xd[H * pos[p] + h], T.L[pos[rank]], T.sem.arr)
+               for p in mine if p != rank for h in hord]
+        near = [(hs[h], T.Xd[H * pos[rank] + h], T.L[pos[rank]], T.sem.arr) for h in hord]
+        room = len(_bits(topo.mask(core, far[0][0])))
+        first = True
+        while far:
+            sent += _fused(g, core, topo, far[:room] + (near if first else []), T.sem.sent)
+            far = far[room:]
+            first = False
+        g.sync.wait_ge(T.sem.yarr, NP)
+        g.sync.dma_start(T.y[:, :], T.Yd[:, :, :]).then_inc(T.sem.st, 16)
+        g.wait_ge(T.sem.sent, sent)
+        g.wait_ge(T.sem.st, 16)
+        return
+
+    own = [r for r in range(N) if core in helpers[r]]
+    if not own:
+        return
+    p = own[0]
+    h = helpers[p].index(core)
+    mine, other = (g0, g1) if p in g0 else (g1, g0)
+
+    _build_matrix(g, T, order)
+
+    sent = 0
+    g.wait_ge(T.sem.hb, len(other))
+    items = [(helpers[d][h], T.Hb[i], T.L[pos[p]], T.sem.arr) for i, d in enumerate(other)]
+    sent += _fused(g, core, topo, items, T.sem.sent)
+    g.sync.wait_ge(T.sem.arr, N)
+    g.sync.dma_start(T.S[:, :], T.L[:, :, :]).then_inc(T.sem.sl, 16)
+    g.tensor.wait_ge(T.sem.mr, 16)
+    g.tensor.wait_ge(T.sem.sl, 16)
+    g.tensor.matmul(T.P[:, :], T.Mx[:, :], T.S[:, :], True, True).then_inc(T.sem.mm, 1)
+    g.vector.wait_ge(T.sem.mm, 1)
+    g.vector.tensor_copy(T.O[:, :], T.P[:, :]).then_inc(T.sem.cp, 1)
+    g.sync.wait_ge(T.sem.cp, 1)
+    g.sync.dma_start(T.Od[:, :, :], T.O[:, :]).then_inc(T.sem.bo, 16)
+    g.wait_ge(T.sem.bo, 16)
+    items = [(cores[r], T.Od[r], T.Yd[H * pos[p] + h], T.sem.yarr) for r in range(N)]
+    sent += _fused(g, core, topo, items, T.sem.sent)
+    g.wait_ge(T.sem.sent, sent)

@@ -21,10 +21,11 @@ W = C // NP
 Q = ROWS // N
 SW = N * W
 XR = ROWS // NP
+G = N // 2
 
 SCRATCH = {
     "Xd": ("dram", [NP, ROWS, W], "bfloat16"),
-    "Hb": ("dram", [N, ROWS, W], "bfloat16"),
+    "Hb": ("dram", [G, ROWS, W], "bfloat16"),
     "L": ("dram", [N, ROWS, W], "bfloat16"),
     "S": ("sbuf", [ROWS, SW], "bfloat16"),
     "A": ("sbuf", [ROWS, ROWS + 1], "bfloat16"),
@@ -35,23 +36,29 @@ SCRATCH = {
     "Od": ("dram", [N, ROWS, W], "bfloat16"),
     "Yd": ("dram", [NP, ROWS, W], "bfloat16"),
 }
-SEMAPHORES = ["ldA", "ldB", "sent", "hb", "arr", "ms", "zs", "mr", "sl", "mm", "cp", "bo", "yarr", "st"]
+SEMAPHORES = (["ldA%d" % k for k in range(H)] + ["yo%d" % k for k in range(H)] + ["ym%d" % k for k in range(H)] +
+              ["ldB", "sent", "hb", "arrE", "arrL", "ms", "zs", "mr", "slE", "slL", "mm", "cp", "boA", "boB", "st"])
 
 
 def _bits(mask):
     return [1 << b for b in range(16) if (mask >> b) & 1]
 
 
-def _fused(g, core, topo, items, local_sem):
+def _fused(g, core, topo, items, local_sem, warm, pool=None):
     groups = {}
     for it in items:
         groups.setdefault(topo.mask(core, it[0]), []).append(it)
     used = set()
     trs = []
     for m in sorted(groups, key=lambda m: len(_bits(m))):
-        free = [e for e in _bits(m) if e not in used]
+        free = [e for e in _bits(m) if e not in used and (pool is None or e in pool)]
         grp = groups[m]
-        step = max(1, len(free) // len(grp))
+        hot = [e for e in free if e in warm]
+        if len(hot) >= len(grp):
+            free = hot
+            step = 1
+        else:
+            step = max(1, len(free) // len(grp))
         for i, (dstc, src, dst, sem) in enumerate(grp):
             e = free[i * step]
             used.add(e)
@@ -59,6 +66,7 @@ def _fused(g, core, topo, items, local_sem):
             trs.append(RemoteDMATransfer(dst_ids=[DstId(rid=rid, pnc=pid)], dma_engine_mask=e,
                                          remote_sem=sem, src=src, dst=dst))
     g.remote_dma_fused(trs, local_sem=local_sem)
+    warm.update(used)
     return len(trs)
 
 
@@ -78,8 +86,8 @@ def _runs(rs):
     return out
 
 
-def _build_matrix(g, T, order):
-    sign = T.tables["SIGN"]
+def _build_matrix(g, T, order, outord):
+    sign = [[T.tables["SIGN"][outord[i]][order[k]] for k in range(N)] for i in range(N)]
     v = g.vector
     n = [0]
 
@@ -97,13 +105,11 @@ def _build_matrix(g, T, order):
     fill(0, ROWS, list(range(N)), 1.0)
     layer()
     for m in range(N // 2):
-        up = order[2 * m + 1]
-        fill(2 * Q * m, 2 * Q * (m + 1), [r for r in range(N) if sign[r][up] < 0], -1.0)
+        fill(2 * Q * m, 2 * Q * (m + 1), [i for i in range(N) if sign[i][2 * m + 1] < 0], -1.0)
     layer()
     for m in range(N // 2):
-        lo, up = order[2 * m], order[2 * m + 1]
         for val in (1, -1):
-            rs = [r for r in range(N) if sign[r][lo] == val and sign[r][up] != val]
+            rs = [i for i in range(N) if sign[i][2 * m] == val and sign[i][2 * m + 1] != val]
             if rs:
                 fill(2 * Q * m, 2 * Q * m + Q, rs, float(val))
     s = g.scalar
@@ -121,44 +127,56 @@ def rank_program(g, core, T, topo):
     order = g0 + g1
     pos = {r: i for i, r in enumerate(order)}
     helpers = {r: [c for c in _port_owners(chips[r]) if c not in cores] for r in range(N)}
+    seen = {}
+    key = {}
+    for h in range(H):
+        d = topo.die(helpers[0][h])
+        key[h] = (seen.get(d, 0), d != topo.die(cores[0]))
+        seen[d] = seen.get(d, 0) + 1
+    hord = sorted(range(H), key=lambda h: key[h])
+    hpos = {h: i for i, h in enumerate(hord)}
+    room = len(_bits(topo.mask(cores[g0[0]], cores[g0[1]])))
+    per = room // G
+
+    def piece(p, h):
+        return (pos[p] // G) * (H * G) + hpos[h] * G + pos[p] % G
 
     rank = T.rank_of(core)
     if rank is not None:
         mine, other = (g0, g1) if rank in g0 else (g1, g0)
         hs = helpers[rank]
-
-        def half(grp):
-            return H * pos[grp[0]], H * pos[grp[-1]] + H
-
-        a0, a1 = half(other)
-        b0, b1 = half(mine)
-        g.sync.dma_start(T.Xd[a0:a1], T.x[XR * a0:XR * a1, :]).then_inc(T.sem.ldA, 16)
-        g.scalar.dma_start(T.Xd[b0:b1], T.x[XR * b0:XR * b1, :]).then_inc(T.sem.ldB, 16)
-        seen = {}
-        key = {}
-        for h in range(H):
-            d = topo.die(hs[h])
-            key[h] = (seen.get(d, 0), d != topo.die(core))
-            seen[d] = seen.get(d, 0) + 1
-        hord = sorted(range(H), key=lambda h: key[h])
-        sent = 0
-        g.wait_ge(T.sem.ldA, 16)
-        items = [(hs[h], T.Xd[H * pos[p] + h], T.Hb[i], T.sem.hb) for i, p in enumerate(other) for h in hord]
-        sent += _fused(g, core, topo, items, T.sem.sent)
-        g.wait_ge(T.sem.ldB, 16)
-        far = [(helpers[p][h], T.Xd[H * pos[p] + h], T.L[pos[rank]], T.sem.arr)
+        far = [(helpers[p][h], T.Xd[piece(p, h)], T.L[pos[rank]], T.sem.arrE)
                for p in mine if p != rank for h in hord]
-        near = [(hs[h], T.Xd[H * pos[rank] + h], T.L[pos[rank]], T.sem.arr) for h in hord]
-        room = len(_bits(topo.mask(core, far[0][0])))
-        first = True
-        while far:
-            sent += _fused(g, core, topo, far[:room] + (near if first else []), T.sem.sent)
-            far = far[room:]
-            first = False
-        g.sync.wait_ge(T.sem.yarr, NP)
-        g.sync.dma_start(T.y[:, :], T.Yd[:, :, :]).then_inc(T.sem.st, 16)
+        near = [(hs[h], T.Xd[piece(rank, h)], T.L[pos[rank]], T.sem.arrE) for h in hord]
+        pool = _bits(topo.mask(core, far[0][0]))
+        queues = [g.sync, g.scalar]
+        a0 = piece(other[0], hord[0])
+        b0 = piece(mine[0], hord[0])
+        for n, k in enumerate(range(0, H, per)):
+            s0, s1 = a0 + k * G, a0 + (k + per) * G
+            queues[n % 2].dma_start(T.Xd[s0:s1], T.x[XR * s0:XR * s1, :]).then_inc(T.sem["ldA%d" % n], 16)
+        g.sync.dma_start(T.Xd[b0:b0 + H * G], T.x[XR * b0:XR * (b0 + H * G), :]).then_inc(T.sem.ldB, 16)
+        sent = 0
+        warm = set()
+        for n, k in enumerate(range(0, H, per)):
+            g.wait_ge(T.sem["ldA%d" % n], 16)
+            items = [(hs[h], T.Xd[piece(p, h)], T.Hb[i], T.sem.hb)
+                     for i, p in enumerate(other) for h in hord[k:k + per]]
+            sent += _fused(g, core, topo, items, T.sem.sent, warm, pool)
+        g.wait_ge(T.sem.ldB, 16)
+        todo = far + near
+        while todo:
+            sent += _fused(g, core, topo, todo[:room], T.sem.sent, warm, pool)
+            todo = todo[room:]
+        stored = 0
+        for q, name, s00 in ((g.sync, "yo%d", a0), (g.scalar, "ym%d", b0)):
+            for n, k in enumerate(range(0, H, per)):
+                s0, s1 = s00 + k * G, s00 + (k + per) * G
+                q.wait_ge(T.sem[name % n], s1 - s0)
+                q.dma_start(T.y[XR * s0:XR * s1, :], T.Yd[s0:s1]).then_inc(T.sem.st, 16)
+                stored += 16
         g.wait_ge(T.sem.sent, sent)
-        g.wait_ge(T.sem.st, 16)
+        g.wait_ge(T.sem.st, stored)
         return
 
     own = [r for r in range(N) if core in helpers[r]]
@@ -167,23 +185,33 @@ def rank_program(g, core, T, topo):
     p = own[0]
     h = helpers[p].index(core)
     mine, other = (g0, g1) if p in g0 else (g1, g0)
+    outord = other + mine
 
-    _build_matrix(g, T, order)
+    _build_matrix(g, T, order, outord)
 
     sent = 0
-    g.wait_ge(T.sem.hb, len(other))
-    items = [(helpers[d][h], T.Hb[i], T.L[pos[p]], T.sem.arr) for i, d in enumerate(other)]
-    sent += _fused(g, core, topo, items, T.sem.sent)
-    g.sync.wait_ge(T.sem.arr, N)
-    g.sync.dma_start(T.S[:, :], T.L[:, :, :]).then_inc(T.sem.sl, 16)
+    warm = set()
+    g.wait_ge(T.sem.hb, G)
+    items = [(helpers[d][h], T.Hb[i], T.L[pos[p]], T.sem.arrL) for i, d in enumerate(other)]
+    sent += _fused(g, core, topo, items, T.sem.sent, warm)
+    e0, l0 = pos[mine[0]], pos[other[0]]
+    g.scalar.wait_ge(T.sem.arrE, G)
+    g.scalar.dma_start(T.S[Q * e0:Q * (e0 + G), :], T.L[e0:e0 + G]).then_inc(T.sem.slE, 16)
+    g.sync.wait_ge(T.sem.arrL, G)
+    g.sync.dma_start(T.S[Q * l0:Q * (l0 + G), :], T.L[l0:l0 + G]).then_inc(T.sem.slL, 16)
     g.tensor.wait_ge(T.sem.mr, 16)
-    g.tensor.wait_ge(T.sem.sl, 16)
+    g.tensor.wait_ge(T.sem.slE, 16)
+    g.tensor.wait_ge(T.sem.slL, 16)
     g.tensor.matmul(T.P[:, :], T.Mx[:, :], T.S[:, :], True, True).then_inc(T.sem.mm, 1)
     g.vector.wait_ge(T.sem.mm, 1)
     g.vector.tensor_copy(T.O[:, :], T.P[:, :]).then_inc(T.sem.cp, 1)
     g.sync.wait_ge(T.sem.cp, 1)
-    g.sync.dma_start(T.Od[:, :, :], T.O[:, :]).then_inc(T.sem.bo, 16)
-    g.wait_ge(T.sem.bo, 16)
-    items = [(cores[r], T.Od[r], T.Yd[H * pos[p] + h], T.sem.yarr) for r in range(N)]
-    sent += _fused(g, core, topo, items, T.sem.sent)
+    g.sync.dma_start(T.Od[0:G], T.O[0:Q * G, :]).then_inc(T.sem.boA, 16)
+    g.scalar.wait_ge(T.sem.cp, 1)
+    g.scalar.dma_start(T.Od[G:N], T.O[Q * G:ROWS, :]).then_inc(T.sem.boB, 16)
+    wave = hpos[h] // per
+    for sem, i0, name in ((T.sem.boA, 0, "yo%d"), (T.sem.boB, G, "ym%d")):
+        g.wait_ge(sem, 16)
+        items = [(cores[outord[i]], T.Od[i], T.Yd[piece(p, h)], T.sem[name % wave]) for i in range(i0, i0 + G)]
+        sent += _fused(g, core, topo, items, T.sem.sent, warm)
     g.wait_ge(T.sem.sent, sent)

@@ -22,9 +22,11 @@ Q = ROWS // N
 SW = N * W
 XR = ROWS // NP
 G = N // 2
+PER = 2
 
 SCRATCH = {
     "Xd": ("dram", [NP, ROWS, W], "bfloat16"),
+    "Rb": ("sbuf", [ROWS, Q], "bfloat16"),
     "Hb": ("dram", [G, ROWS, W], "bfloat16"),
     "L": ("dram", [N, ROWS, W], "bfloat16"),
     "S": ("sbuf", [ROWS, SW], "bfloat16"),
@@ -36,8 +38,10 @@ SCRATCH = {
     "Od": ("dram", [N, ROWS, W], "bfloat16"),
     "Yd": ("dram", [NP, ROWS, W], "bfloat16"),
 }
-SEMAPHORES = (["ldA%d" % k for k in range(H)] + ["yo%d" % k for k in range(H)] + ["ym%d" % k for k in range(H)] +
-              ["ldB", "sent", "hb", "arrE", "arrL", "ms", "zs", "mr", "slE", "slL", "mm", "cp", "boA", "boB", "st"])
+SEMAPHORES = (["ldA%d" % k for k in range(H // PER)] + ["yo%d" % k for k in range(H // PER)] +
+              ["ym%d" % k for k in range(H // PER)] +
+              ["ldB", "rs", "sent", "hb", "arrE", "arrL", "ms", "ax", "ar", "zs", "mr", "slE", "slL", "mm", "cp",
+               "boA", "boB", "st"])
 
 
 def _bits(mask):
@@ -54,13 +58,12 @@ def _fused(g, core, topo, items, local_sem, warm, pool=None):
         free = [e for e in _bits(m) if e not in used and (pool is None or e in pool)]
         grp = groups[m]
         hot = [e for e in free if e in warm]
-        if len(hot) >= len(grp):
-            free = hot
-            step = 1
+        if hot:
+            pick = hot + [e for e in free if e not in warm]
         else:
-            step = max(1, len(free) // len(grp))
+            pick = free[::max(1, len(free) // len(grp))]
         for i, (dstc, src, dst, sem) in enumerate(grp):
-            e = free[i * step]
+            e = pick[i]
             used.add(e)
             rid, pid, _se = topo.addr(dstc)
             trs.append(RemoteDMATransfer(dst_ids=[DstId(rid=rid, pnc=pid)], dma_engine_mask=e,
@@ -86,8 +89,7 @@ def _runs(rs):
     return out
 
 
-def _build_matrix(g, T, order, outord):
-    sign = [[T.tables["SIGN"][outord[i]][order[k]] for k in range(N)] for i in range(N)]
+def _fill(g, T, sign, lo, hi, c0, c1):
     v = g.vector
     n = [0]
 
@@ -99,24 +101,20 @@ def _build_matrix(g, T, order, outord):
     def layer():
         v.wait_ge(T.sem.ms, n[0])
 
-    v.memset(T.A[:, :], 0.0).then_inc(T.sem.ms, 1)
+    v.memset(T.A[:, c0:c1], 0.0).then_inc(T.sem.ms, 1)
     n[0] += 1
     layer()
-    fill(0, ROWS, list(range(N)), 1.0)
+    fill(0, ROWS, list(range(lo, hi)), 1.0)
     layer()
     for m in range(N // 2):
-        fill(2 * Q * m, 2 * Q * (m + 1), [i for i in range(N) if sign[i][2 * m + 1] < 0], -1.0)
+        fill(2 * Q * m, 2 * Q * (m + 1), [i for i in range(lo, hi) if sign[i][2 * m + 1] < 0], -1.0)
     layer()
     for m in range(N // 2):
         for val in (1, -1):
-            rs = [i for i in range(N) if sign[i][2 * m] == val and sign[i][2 * m + 1] != val]
+            rs = [i for i in range(lo, hi) if sign[i][2 * m] == val and sign[i][2 * m + 1] != val]
             if rs:
                 fill(2 * Q * m, 2 * Q * m + Q, rs, float(val))
-    s = g.scalar
-    s.wait_ge(T.sem.ms, n[0])
-    s.dma_start(T.Z[:, :], T.A[:, :]).then_inc(T.sem.zs, 16)
-    s.wait_ge(T.sem.zs, 16)
-    s.dma_start(T.Mx[:, :], T.Z[:, 0:Q * ROWS]).then_inc(T.sem.mr, 16)
+    return n[0]
 
 
 def rank_program(g, core, T, topo):
@@ -135,43 +133,59 @@ def rank_program(g, core, T, topo):
         seen[d] = seen.get(d, 0) + 1
     hord = sorted(range(H), key=lambda h: key[h])
     hpos = {h: i for i, h in enumerate(hord)}
-    room = len(_bits(topo.mask(cores[g0[0]], cores[g0[1]])))
-    per = room // G
+    waves = H // PER
 
     def piece(p, h):
         return (pos[p] // G) * (H * G) + hpos[h] * G + pos[p] % G
 
+    def signs(outord):
+        sign = [[T.tables["SIGN"][outord[i]][order[k]] for k in range(N)] for i in range(N)]
+        return sign, [i for i in range(N) if min(sign[i]) > 0][0]
+
     rank = T.rank_of(core)
     if rank is not None:
         mine, other = (g0, g1) if rank in g0 else (g1, g0)
+        away = [p for p in mine if p != rank]
         hs = helpers[rank]
-        far = [(helpers[p][h], T.Xd[piece(p, h)], T.L[pos[rank]], T.sem.arrE)
-               for p in mine if p != rank for h in hord]
-        near = [(hs[h], T.Xd[piece(rank, h)], T.L[pos[rank]], T.sem.arrE) for h in hord]
-        pool = _bits(topo.mask(core, far[0][0]))
-        queues = [g.sync, g.scalar]
+        pool = _bits(topo.mask(core, cores[away[0]]))
         a0 = piece(other[0], hord[0])
         b0 = piece(mine[0], hord[0])
-        for n, k in enumerate(range(0, H, per)):
-            s0, s1 = a0 + k * G, a0 + (k + per) * G
+        queues = [g.sync, g.scalar]
+        for n in range(waves):
+            s0, s1 = a0 + n * PER * G, a0 + (n + 1) * PER * G
             queues[n % 2].dma_start(T.Xd[s0:s1], T.x[XR * s0:XR * s1, :]).then_inc(T.sem["ldA%d" % n], 16)
         g.sync.dma_start(T.Xd[b0:b0 + H * G], T.x[XR * b0:XR * (b0 + H * G), :]).then_inc(T.sem.ldB, 16)
+        _sign, plus = signs(other + mine)
+        g.vector.memset(T.Rb[:, 0:1], 1.0).then_inc(T.sem.rs, 1)
+        g.vector.memset(T.Rb[:, 1:Q], 0.0).then_inc(T.sem.rs, 1)
         sent = 0
         warm = set()
-        for n, k in enumerate(range(0, H, per)):
+        ne = len(pool) // H
+        trs = []
+        for i, h in enumerate(hord):
+            rid, pid, _se = topo.addr(hs[h])
+            es = pool[ne * i:ne * (i + 1)]
+            trs.append(RemoteDMATransfer(dst_ids=[DstId(rid=rid, pnc=pid)], dma_engine_mask=sum(es),
+                                         remote_sem=T.sem.ar, src=T.Rb[:, :], dst=T.A[:, Q * plus:Q * (plus + 1)]))
+            warm.update(es)
+            sent += len(es)
+        g.wait_ge(T.sem.rs, 2)
+        g.remote_dma_fused(trs, local_sem=T.sem.sent)
+        for n in range(waves):
             g.wait_ge(T.sem["ldA%d" % n], 16)
             items = [(hs[h], T.Xd[piece(p, h)], T.Hb[i], T.sem.hb)
-                     for i, p in enumerate(other) for h in hord[k:k + per]]
+                     for i, p in enumerate(other) for h in hord[n * PER:(n + 1) * PER]]
             sent += _fused(g, core, topo, items, T.sem.sent, warm, pool)
         g.wait_ge(T.sem.ldB, 16)
-        todo = far + near
+        todo = ([(helpers[p][h], T.Xd[piece(p, h)], T.L[pos[rank]], T.sem.arrE) for p in away for h in hord] +
+                [(hs[h], T.Xd[piece(rank, h)], T.L[pos[rank]], T.sem.arrE) for h in hord])
         while todo:
-            sent += _fused(g, core, topo, todo[:room], T.sem.sent, warm, pool)
-            todo = todo[room:]
+            sent += _fused(g, core, topo, todo[:len(pool)], T.sem.sent, warm, pool)
+            todo = todo[len(pool):]
         stored = 0
         for q, name, s00 in ((g.sync, "yo%d", a0), (g.scalar, "ym%d", b0)):
-            for n, k in enumerate(range(0, H, per)):
-                s0, s1 = s00 + k * G, s00 + (k + per) * G
+            for n in range(waves):
+                s0, s1 = s00 + n * PER * G, s00 + (n + 1) * PER * G
                 q.wait_ge(T.sem[name % n], s1 - s0)
                 q.dma_start(T.y[XR * s0:XR * s1, :], T.Yd[s0:s1]).then_inc(T.sem.st, 16)
                 stored += 16
@@ -186,11 +200,31 @@ def rank_program(g, core, T, topo):
     h = helpers[p].index(core)
     mine, other = (g0, g1) if p in g0 else (g1, g0)
     outord = other + mine
+    off = _bits(topo.mask(core, cores[other[0]]))
+    eng = off[::len(off) // G][:G]
 
-    _build_matrix(g, T, order, outord)
-
+    sign, plus = signs(outord)
+    half = hpos[h] % PER
+    lo, hi = (0, N // 2) if half == 0 else (N // 2, N)
+    c1 = Q * hi if half == 0 else ROWS + 1
+    if lo == plus:
+        lo += 1
+    c0 = Q * lo
+    nfill = _fill(g, T, sign, lo, hi, c0, c1)
     sent = 0
-    warm = set()
+    warm = set(eng)
+    rid, pid, _se = topo.addr(helpers[p][hord[hpos[h] ^ 1]])
+    g.wait_ge(T.sem.ms, nfill)
+    g.remote_dma(T.A[:, c0:c1], T.A[:, c0:c1], T.sem.ax, T.sem.sent, pid, rid, sum(eng))
+    sent += len(eng)
+    s = g.scalar
+    s.wait_ge(T.sem.ms, nfill)
+    s.wait_ge(T.sem.ax, len(eng))
+    s.wait_ge(T.sem.ar, len(_bits(topo.mask(cores[p], cores[other[0]]))) // H)
+    s.dma_start(T.Z[:, :], T.A[:, :]).then_inc(T.sem.zs, 16)
+    s.wait_ge(T.sem.zs, 16)
+    s.dma_start(T.Mx[:, :], T.Z[:, 0:Q * ROWS]).then_inc(T.sem.mr, 16)
+
     g.wait_ge(T.sem.hb, G)
     items = [(helpers[d][h], T.Hb[i], T.L[pos[p]], T.sem.arrL) for i, d in enumerate(other)]
     sent += _fused(g, core, topo, items, T.sem.sent, warm)
@@ -209,7 +243,7 @@ def rank_program(g, core, T, topo):
     g.sync.dma_start(T.Od[0:G], T.O[0:Q * G, :]).then_inc(T.sem.boA, 16)
     g.scalar.wait_ge(T.sem.cp, 1)
     g.scalar.dma_start(T.Od[G:N], T.O[Q * G:ROWS, :]).then_inc(T.sem.boB, 16)
-    wave = hpos[h] // per
+    wave = hpos[h] // PER
     for sem, i0, name in ((T.sem.boA, 0, "yo%d"), (T.sem.boB, G, "ym%d")):
         g.wait_ge(sem, 16)
         items = [(cores[outord[i]], T.Od[i], T.Yd[piece(p, h)], T.sem[name % wave]) for i in range(i0, i0 + G)]

import comms_topo
from concourse.bass import DstId, RemoteDMATransfer

N = 8
ROWS = 128
C = 1024


def _all_cores():
    return range(comms_topo.CHIPS * comms_topo.CORES_PER_CHIP)


def _port_owners(ch):
    far = [c for c in _all_cores() if comms_topo.mates(ch, comms_topo.chip(c))][0]
    return [c for c in _all_cores() if comms_topo.chip(c) == ch and comms_topo.may_write(c, far)]


H = len(_port_owners(0))
NP = N * H
W = C // NP
Q = ROWS // N
SW = N * W
XR = ROWS // NP
G = N // 2
PER = 2

SCRATCH = {
    "Xd": ("dram", [NP, ROWS, W], "bfloat16"),
    "Rb": ("sbuf", [ROWS, Q], "bfloat16"),
    "Hb": ("dram", [G, ROWS, W], "bfloat16"),
    "L": ("dram", [N, ROWS, W], "bfloat16"),
    "S": ("sbuf", [ROWS, SW], "bfloat16"),
    "A": ("sbuf", [ROWS, ROWS + 1], "bfloat16"),
    "Z": ("dram", [N, Q * (ROWS + 1)], "bfloat16"),
    "Mx": ("sbuf", [ROWS, ROWS], "bfloat16"),
    "P": ("psum", [ROWS, SW], "float32"),
    "O": ("sbuf", [ROWS, SW], "bfloat16"),
    "Od": ("dram", [N, ROWS, W], "bfloat16"),
    "Yd": ("dram", [NP, ROWS, W], "bfloat16"),
}
SEMAPHORES = (["ldA%d" % k for k in range(H // PER)] + ["yo%d" % k for k in range(H // PER)] +
              ["ym%d" % k for k in range(H // PER)] +
              ["ldB", "rs", "sent", "hb", "arrE", "arrL", "ms", "ax", "ar", "zs", "mr", "slE", "slL", "mm", "cp",
               "boA", "boB", "st"])


def _bits(mask):
    return [1 << b for b in range(16) if (mask >> b) & 1]


def _fused(g, core, topo, items, local_sem, warm, pool=None):
    groups = {}
    for it in items:
        groups.setdefault(topo.mask(core, it[0]), []).append(it)
    used = set()
    trs = []
    for m in sorted(groups, key=lambda m: len(_bits(m))):
        free = [e for e in _bits(m) if e not in used and (pool is None or e in pool)]
        grp = groups[m]
        hot = [e for e in free if e in warm]
        if hot:
            pick = hot + [e for e in free if e not in warm]
        else:
            pick = free[::max(1, len(free) // len(grp))]
        for i, (dstc, src, dst, sem) in enumerate(grp):
            e = pick[i]
            used.add(e)
            rid, pid, _se = topo.addr(dstc)
            trs.append(RemoteDMATransfer(dst_ids=[DstId(rid=rid, pnc=pid)], dma_engine_mask=e,
                                         remote_sem=sem, src=src, dst=dst))
    g.remote_dma_fused(trs, local_sem=local_sem)
    warm.update(used)
    return len(trs)


def _runs(rs):
    rs = list(rs)
    out = []
    while rs:
        if len(rs) == 1:
            out.append((rs[0], 1, 1))
            break
        step = rs[1] - rs[0]
        n = 2
        while n < len(rs) and rs[n] - rs[n - 1] == step:
            n += 1
        out.append((rs[0], step, n))
        rs = rs[n:]
    return out


def _fill(g, T, sign, lo, hi, c0, c1):
    v = g.vector
    n = [0]

    def fill(p0, p1, rs, val):
        for (a, step, cnt) in _runs(rs):
            v.memset(T.A[p0:p1, Q * a:Q * (a + step * (cnt - 1)) + 1:Q * step], val).then_inc(T.sem.ms, 1)
            n[0] += 1

    def layer():
        v.wait_ge(T.sem.ms, n[0])

    v.memset(T.A[:, c0:c1], 0.0).then_inc(T.sem.ms, 1)
    n[0] += 1
    layer()
    fill(0, ROWS, list(range(lo, hi)), 1.0)
    layer()
    for m in range(N // 2):
        fill(2 * Q * m, 2 * Q * (m + 1), [i for i in range(lo, hi) if sign[i][2 * m + 1] < 0], -1.0)
    layer()
    for m in range(N // 2):
        for val in (1, -1):
            rs = [i for i in range(lo, hi) if sign[i][2 * m] == val and sign[i][2 * m + 1] != val]
            if rs:
                fill(2 * Q * m, 2 * Q * m + Q, rs, float(val))
    return n[0]


def rank_program(g, core, T, topo):
    cores = list(T.cores)
    chips = [topo.chip(c) for c in cores]
    g0 = [r for r in range(N) if chips[r] == chips[0] or topo.same_plane(chips[r], chips[0])]
    g1 = [r for r in range(N) if r not in g0]
    order = g0 + g1
    pos = {r: i for i, r in enumerate(order)}
    helpers = {r: [c for c in _port_owners(chips[r]) if c not in cores] for r in range(N)}
    seen = {}
    key = {}
    for h in range(H):
        d = topo.die(helpers[0][h])
        key[h] = (seen.get(d, 0), d != topo.die(cores[0]))
        seen[d] = seen.get(d, 0) + 1
    hord = sorted(range(H), key=lambda h: key[h])
    hpos = {h: i for i, h in enumerate(hord)}
    waves = H // PER

    def piece(p, h):
        return (pos[p] // G) * (H * G) + hpos[h] * G + pos[p] % G

    def signs(outord):
        sign = [[T.tables["SIGN"][outord[i]][order[k]] for k in range(N)] for i in range(N)]
        return sign, [i for i in range(N) if min(sign[i]) > 0][0]

    rank = T.rank_of(core)
    if rank is not None:
        mine, other = (g0, g1) if rank in g0 else (g1, g0)
        away = [p for p in mine if p != rank]
        hs = helpers[rank]
        pool = _bits(topo.mask(core, cores[away[0]]))
        a0 = piece(other[0], hord[0])
        b0 = piece(mine[0], hord[0])
        queues = [g.sync, g.scalar]
        for n in range(waves):
            s0, s1 = a0 + n * PER * G, a0 + (n + 1) * PER * G
            queues[n % 2].dma_start(T.Xd[s0:s1], T.x[XR * s0:XR * s1, :]).then_inc(T.sem["ldA%d" % n], 16)
        g.sync.dma_start(T.Xd[b0:b0 + H * G], T.x[XR * b0:XR * (b0 + H * G), :]).then_inc(T.sem.ldB, 16)
        _sign, plus = signs(other + mine)
        g.vector.memset(T.Rb[:, 0:1], 1.0).then_inc(T.sem.rs, 1)
        g.vector.memset(T.Rb[:, 1:Q], 0.0).then_inc(T.sem.rs, 1)
        sent = 0
        warm = set()
        ne = len(pool) // H
        trs = []
        for i, h in enumerate(hord):
            rid, pid, _se = topo.addr(hs[h])
            es = pool[ne * i:ne * (i + 1)]
            trs.append(RemoteDMATransfer(dst_ids=[DstId(rid=rid, pnc=pid)], dma_engine_mask=sum(es),
                                         remote_sem=T.sem.ar, src=T.Rb[:, :], dst=T.A[:, Q * plus:Q * (plus + 1)]))
            warm.update(es)
            sent += len(es)
        g.wait_ge(T.sem.rs, 2)
        g.remote_dma_fused(trs, local_sem=T.sem.sent)
        for n in range(waves):
            g.wait_ge(T.sem["ldA%d" % n], 16)
            items = [(hs[h], T.Xd[piece(p, h)], T.Hb[i], T.sem.hb)
                     for i, p in enumerate(other) for h in hord[n * PER:(n + 1) * PER]]
            sent += _fused(g, core, topo, items, T.sem.sent, warm, pool)
        g.wait_ge(T.sem.ldB, 16)
        todo = ([(helpers[p][h], T.Xd[piece(p, h)], T.L[pos[rank]], T.sem.arrE) for p in away for h in hord] +
                [(hs[h], T.Xd[piece(rank, h)], T.L[pos[rank]], T.sem.arrE) for h in hord])
        while todo:
            sent += _fused(g, core, topo, todo[:len(pool)], T.sem.sent, warm, pool)
            todo = todo[len(pool):]
        stored = 0
        for q, name, s00 in ((g.sync, "yo%d", a0), (g.scalar, "ym%d", b0)):
            for n in range(waves):
                s0, s1 = s00 + n * PER * G, s00 + (n + 1) * PER * G
                q.wait_ge(T.sem[name % n], s1 - s0)
                q.dma_start(T.y[XR * s0:XR * s1, :], T.Yd[s0:s1]).then_inc(T.sem.st, 16)
                stored += 16
        g.wait_ge(T.sem.sent, sent)
        g.wait_ge(T.sem.st, stored)
        return

    own = [r for r in range(N) if core in helpers[r]]
    if not own:
        return
    p = own[0]
    h = helpers[p].index(core)
    mine, other = (g0, g1) if p in g0 else (g1, g0)
    outord = other + mine
    off = _bits(topo.mask(core, cores[other[0]]))
    eng = off[::len(off) // G][:G]

    sign, plus = signs(outord)
    half = hpos[h] % PER
    lo, hi = (0, N // 2) if half == 0 else (N // 2, N)
    c1 = Q * hi if half == 0 else ROWS + 1
    if lo == plus:
        lo += 1
    c0 = Q * lo
    nfill = _fill(g, T, sign, lo, hi, c0, c1)
    sent = 0
    warm = set(eng)
    rid, pid, _se = topo.addr(helpers[p][hord[hpos[h] ^ 1]])
    g.wait_ge(T.sem.ms, nfill)
    g.remote_dma(T.A[:, c0:c1], T.A[:, c0:c1], T.sem.ax, T.sem.sent, pid, rid, sum(eng))
    sent += len(eng)
    s = g.scalar
    s.wait_ge(T.sem.ms, nfill)
    s.wait_ge(T.sem.ax, len(eng))
    s.wait_ge(T.sem.ar, len(_bits(topo.mask(cores[p], cores[other[0]]))) // H)
    s.dma_start(T.Z[:, :], T.A[:, :]).then_inc(T.sem.zs, 16)
    s.wait_ge(T.sem.zs, 16)
    s.dma_start(T.Mx[:, :], T.Z[:, 0:Q * ROWS]).then_inc(T.sem.mr, 16)

    g.wait_ge(T.sem.hb, G)
    items = [(helpers[d][h], T.Hb[i], T.L[pos[p]], T.sem.arrL) for i, d in enumerate(other)]
    sent += _fused(g, core, topo, items, T.sem.sent, warm)
    e0, l0 = pos[mine[0]], pos[other[0]]
    g.scalar.wait_ge(T.sem.arrE, G)
    g.scalar.dma_start(T.S[Q * e0:Q * (e0 + G), :], T.L[e0:e0 + G]).then_inc(T.sem.slE, 16)
    g.sync.wait_ge(T.sem.arrL, G)
    g.sync.dma_start(T.S[Q * l0:Q * (l0 + G), :], T.L[l0:l0 + G]).then_inc(T.sem.slL, 16)
    g.tensor.wait_ge(T.sem.mr, 16)
    g.tensor.wait_ge(T.sem.slE, 16)
    g.tensor.wait_ge(T.sem.slL, 16)
    g.tensor.matmul(T.P[:, :], T.Mx[:, :], T.S[:, :], True, True).then_inc(T.sem.mm, 1)
    g.vector.wait_ge(T.sem.mm, 1)
    g.vector.tensor_copy(T.O[:, :], T.P[:, :]).then_inc(T.sem.cp, 1)
    g.sync.wait_ge(T.sem.cp, 1)
    g.sync.dma_start(T.Od[0:G], T.O[0:Q * G, :]).then_inc(T.sem.boA, 16)
    g.scalar.wait_ge(T.sem.cp, 1)
    g.scalar.dma_start(T.Od[G:N], T.O[Q * G:ROWS, :]).then_inc(T.sem.boB, 16)
    wave = hpos[h] // PER
    for sem, i0, name in ((T.sem.boA, 0, "yo%d"), (T.sem.boB, G, "ym%d")):
        g.wait_ge(sem, 16)
        items = [(cores[outord[i]], T.Od[i], T.Yd[piece(p, h)], T.sem[name % wave]) for i in range(i0, i0 + G)]
        sent += _fused(g, core, topo, items, T.sem.sent, warm)
    g.wait_ge(T.sem.sent, sent)
